import numpy as np
import ml_dtypes


def mxq(x, axis, fmt="e4m3"):
    dtype, down = {"e4m3": (ml_dtypes.float8_e4m3fn, 7), "e5m2": (ml_dtypes.float8_e5m2, 14)}[fmt]
    v = np.moveaxis(np.asarray(x, np.float32).astype(ml_dtypes.bfloat16).astype(np.float64), axis, -1)
    blocks = v.reshape(v.shape[:-1] + (-1, 32))
    amax = np.abs(blocks).max(-1, keepdims=True)
    byte = np.maximum(np.where(amax > 0, np.frexp(amax)[1] - 1 + 127, 0) - down, 1)
    scale = np.exp2(byte - 127.0)
    codes = (blocks / scale).astype(np.float32).astype(dtype).astype(np.float64)
    return np.moveaxis((codes * scale).reshape(v.shape), -1, axis)


WIDE = False


def mx_kscale(k):
    if not WIDE:
        return np.ones(k)
    levels = np.array([10, -10, 5, -5, 0])
    if k % 512:
        return np.exp2(np.random.permutation(np.resize(levels, k // 32))).repeat(32)
    a = np.empty((k // 512, 16))
    for p in range(k // 512):
        a[p, :8] = np.random.permutation(np.resize(levels, 8))
        for g in range(8):
            far = levels[np.abs(levels - a[p, g]) >= 10]
            a[p, g + 8] = far[np.random.randint(len(far))]
    return np.exp2(a.ravel()).repeat(32)


def f64(x):
    return np.asarray(x).astype(np.float64)


def striped(idx):
    return np.tile(np.asarray(idx).reshape(-1, 16).T, (8, 1)).astype(np.uint16)


def unstriped(offs):
    return offs[:16].T.reshape(-1).astype(np.int64)


E2M1 = np.array([0.0, 0.5, 1.0, 1.5, 2.0, 3.0, 4.0, 6.0, -0.0, -0.5, -1.0, -1.5, -2.0, -3.0, -4.0, -6.0])


def pack_weight(w, fmt):
    k, n = w.shape
    w = f64(np.asarray(w, np.float32).astype(ml_dtypes.bfloat16)).reshape(k // 32, 32, n)
    amax = np.abs(w).max(1)
    if fmt == "e4m3":
        byte = np.frexp(amax)[1] - 1 + 127 - 7
    else:
        mant, ex = np.frexp(amax / 6.0)
        byte = np.where(mant > 0.5, ex, ex - 1) + 127
    byte = np.clip(np.where(amax > 0, byte, 1), 1, 254)
    scaled = (w * np.exp2(127.0 - byte)[:, None, :]).reshape(k, n).astype(np.float32)
    by_word = np.ascontiguousarray(scaled.reshape(k // 512, 128, 4, n).transpose(0, 1, 3, 2))
    if fmt == "e4m3":
        words = by_word.astype(ml_dtypes.float8_e4m3fn).view(np.uint8)
    else:
        c = by_word.astype(ml_dtypes.float4_e2m1fn).view(np.uint8) & 0xF
        words = (c[..., 0::2] | (c[..., 1::2] << 4)).reshape(k // 512, 128, 2 * n)
    return np.ascontiguousarray(words), np.ascontiguousarray(byte.astype(np.uint8).reshape(k // 512, 16, n))


def unpack_weight(words, scales, fmt):
    g, _, n = scales.shape
    words = np.ascontiguousarray(words).reshape(g, 128, n, -1)
    if fmt == "e4m3":
        vals = words.view(ml_dtypes.float8_e4m3fn).astype(np.float64)
    else:
        nib = np.empty((g, 128, n, 4), np.uint8)
        nib[..., 0::2] = words & 0xF
        nib[..., 1::2] = words >> 4
        vals = E2M1[nib]
    vals = vals * np.repeat(np.exp2(scales.astype(np.float64) - 127.0), 8, axis=1)[..., None]
    return vals.transpose(0, 1, 3, 2).reshape(g * 512, n)


def sigmoid(v):
    return 1.0 / (1.0 + np.exp(-v))


D, E, T, I, Q, G, U = 512, 512, 2048, 512, 128, 64, 256


def setup_inputs():
    n = np.random.standard_normal
    idx2 = np.random.permutation(U)[:G]
    idx = np.random.permutation(T)[:I]
    fd = mx_kscale(D)
    fe = mx_kscale(E)
    keysp = pack_weight(n((D, T)) / fd[:, None], "e2m1")
    valsp = pack_weight(n((E, T)) / fe[:, None], "e2m1")
    return {
        "query": (n((D, Q)) * 0.7 / np.sqrt(D) * fd[:, None]).astype(np.float32),
        "pquery": (n((D, Q)) * 1.0 / np.sqrt(D) * fd[:, None]).astype(np.float32),
        "keys_words": keysp[0],
        "keys_scales": keysp[1],
        "pgsum": (n((D, U)) / fd[:, None]).astype(np.float32),
        "reserve": (np.random.uniform(20.0, 100.0, (Q, 1))).astype(np.float32),
        "gout": (n((E, Q)) * 1 / np.sqrt(E) * fe[:, None]).astype(np.float32),
        "vals_words": valsp[0],
        "vals_scales": valsp[1],
        "base": (0.5 * n((Q, I))).astype(np.float32),
        "offs2": striped(idx2),
        "offs": striped(idx),
    }


def reference(query, pquery, keys_words, keys_scales, pgsum, reserve, gout, vals_words, vals_scales, base, offs2, offs):
    idx2 = unstriped(offs2)
    idx = unstriped(offs)
    keysu = unpack_weight(keys_words, keys_scales, "e2m1")
    valsu = unpack_weight(vals_words, vals_scales, "e2m1")
    pqueryq = mxq(f64(pquery), 0, "e4m3")
    pgsumidx2q = mxq(f64(pgsum)[:, idx2], 0, "e4m3")
    h0 = pqueryq.T @ pgsumidx2q
    g1 = sigmoid(h0)
    gr = np.repeat(g1, I // G, axis=1)
    queryq = mxq(f64(query), 0, "e4m3")
    keysidxg = keysu[:, idx]
    a = queryq.T @ keysidxg
    p = np.exp(a) * gr
    z = np.sum(p, axis=1, keepdims=True) + f64(reserve)
    goutq = mxq(f64(gout), 0, "e4m3")
    valsidxg = valsu[:, idx]
    c0 = goutq.T @ valsidxg
    dz = np.sum(c0 * p / np.square(z) * (-1.0), axis=1, keepdims=True)
    dp = c0 / z + dz
    da = dp * gr * np.exp(a)
    hda = da * 512.0 * 2.0 * 512.0
    hdp = hda * np.exp(a) * gr
    hdz = np.sum(hdp, axis=1, keepdims=True)
    hz = np.sum(hdp * c0 / np.square(z) * (-1.0), axis=1, keepdims=True) + np.sum(hdz * (-1.0) * c0 * p / np.square(np.square(z)) * (-1.0), axis=1, keepdims=True) * z * 2.0
    hp = hdz * (-1.0) / np.square(z) * c0 + hz
    ha = hda * dp * gr * np.exp(a) + hp * gr * np.exp(a)
    y = ha + f64(base)
    return y

@@ -1,0 +1,156 @@
+import math
+from contextlib import ExitStack
+
+import concourse.mybir as mybir
+
+D, T, I, Q, G, U = 512, 2048, 512, 128, 64, 256
+FLOPS = 2 * D * Q * (G + 2 * I)
+
+F32 = mybir.dt.float32
+BF16 = mybir.dt.bfloat16
+I32 = mybir.dt.int32
+U32 = mybir.dt.uint32
+U16 = mybir.dt.uint16
+U8 = mybir.dt.uint8
+FP8X4 = mybir.dt.float8_e4m3fn_x4
+FP4X4 = mybir.dt.float4_e2m1fn_x4
+ALU = mybir.AluOpType
+ACT = mybir.ActivationFunctionType
+
+P = 128
+PACK = 4
+PAGE = I // G
+ROOT_K = math.sqrt(512.0 * 2.0 * 512.0)
+
+
+def tile_attend_gppagetablegate_kernel(tc, query, pquery, keys_words, keys_scales, pgsum, reserve, gout,
+                                        vals_words, vals_scales, base, offs2, offs, out):
+    nc = tc.nc
+    with ExitStack() as ctx:
+        sb = ctx.enter_context(tc.tile_pool(name="sb", bufs=1))
+        ps = ctx.enter_context(tc.psum_pool(name="ps", bufs=1))
+
+        def tile(name, shape, dtype):
+            return sb.tile(shape, dtype, name=name, align_bytes=64)
+
+        tokens = sb.tile([P, I // 16], U16, name="tokens")
+        pages = sb.tile([P, G // 16], U16, name="pages")
+        k_words = tile("k_words", [P, T], U16)
+        v_words = tile("v_words", [P, T], U16)
+        k_scales = tile("k_scales", [P, T], U8)
+        v_scales = tile("v_scales", [P, T], U8)
+        q_raw = tile("q_raw", [P, PACK, Q], F32)
+        pq_raw = tile("pq_raw", [P, PACK, Q], F32)
+        go_raw = tile("go_raw", [P, PACK, Q], F32)
+        pg_raw = tile("pg_raw", [P, PACK * U], F32)
+        base_sb = tile("base_sb", [P, I], F32)
+        reserve_sb = tile("reserve_sb", [P, 1], F32)
+        gate = tile("gate", [P, G + 1, 1], F32)
+
+        def load_scales(plane, scales, queue):
+            rows = scales[0].bitcast(I32).rearrange("(s r) c -> r s c", r=4)
+            for r in range(4):
+                queue.dma_start(out=plane[:].bitcast(I32)[r:P:32, :], in_=rows[r])
+
+        def planes(x):
+            return x.rearrange("(p j) w -> p j w", j=PACK)
+
+        spread = tile("spread", [P, 1], F32)
+        nc.vector.memset(k_scales[:].bitcast(I32), 0)
+        nc.vector.memset(spread[:], -0.75)
+        nc.vector.memset(v_scales[:].bitcast(I32), 0)
+        nc.sync.dma_start(tokens[:], offs)
+        nc.sync.dma_start(out=k_words[:].bitcast(I32), in_=keys_words[0].bitcast(I32))
+        load_scales(k_scales, keys_scales, nc.scalar)
+        nc.scalar.activation(gate[:, G, :], spread[:], ACT.Copy)
+        nc.sync.dma_start(out=pg_raw[:], in_=pgsum.rearrange("(p j) w -> p (j w)", j=PACK))
+        nc.sync.dma_start(pages[:], offs2)
+        nc.sync.dma_start(out=pq_raw[:], in_=planes(pquery))
+        nc.sync.dma_start(out=q_raw[:], in_=planes(query))
+        load_scales(v_scales, vals_scales, nc.sync)
+        nc.sync.dma_start(out=v_words[:].bitcast(I32), in_=vals_words[0].bitcast(I32))
+        nc.sync.dma_start(out=go_raw[:], in_=planes(gout))
+        nc.sync.dma_start(out=reserve_sb[:], in_=reserve)
+        nc.sync.dma_start(out=base_sb[:], in_=base)
+
+        def gather(name, window, dtype):
+            picked = tile(name, [P, I], dtype)
+            nc.vector.tensor_copy(picked[:], window[:].indirect(tokens[:]))
+            return picked
+
+        def quantize(name, grouped, width):
+            codes = tile(name + "_codes", [P, width], U32)
+            scales = tile(name + "_scales", [P, width], U8)
+            nc.vector.quantize_mx(out=codes[:].bitcast(FP8X4), scales=scales[:],
+                                  in_=grouped[:].rearrange("p w j -> p (w j)"))
+            return codes, scales
+
+        def interleave(name, raw):
+            grouped = tile(name + "_grouped", [P, Q, PACK], BF16)
+            nc.scalar.copy(out=grouped[:].rearrange("p (c i) j -> p c j i", i=4),
+                           in_=raw[:].rearrange("p j (c i) -> p c j i", i=4))
+            return grouped
+
+        def product(name, rows, words, word_dtype, scales, width):
+            acc = ps.tile([P, width], F32, name=name)
+            nc.tensor.matmul_mx(out=acc[:], lhsT=rows[0][:].bitcast(FP8X4), lhsT_scale=rows[1][:],
+                                rhs=words[:].bitcast(word_dtype), rhs_scale=scales[:], start=True, stop=True)
+            return acc
+
+        kg_scales = gather("kg_scales", k_scales, U8)
+        kg_words = gather("kg_words", k_words, U16)
+
+        pg_grouped = tile("pg_grouped", [P, G, PACK], BF16)
+        for j in range(PACK):
+            nc.vector.tensor_copy(pg_grouped[:, :, j], pg_raw[:, j * U:(j + 1) * U].indirect(pages[:]))
+        pg_codes, pg_scales = quantize("pg", pg_grouped, G)
+        pq_mx = quantize("pq", interleave("pq", pq_raw), Q)
+        h0 = product("h0", pq_mx, pg_codes, FP8X4, pg_scales, G)
+        nc.scalar.activation(gate[:, 0:G, 0], h0[:], ACT.Tanh, scale=0.5)
+
+        q_mx = quantize("q", interleave("q", q_raw), Q)
+        a = product("a", q_mx, kg_words, FP4X4, kg_scales, I)
+        e = tile("e", [P, I + PAGE], F32)
+        nc.scalar.activation(e[:, I:], reserve_sb[:].to_broadcast([P, PAGE]), ACT.Copy)
+        nc.scalar.activation(e[:, 0:I], a[:], ACT.Exp)
+
+        vg_scales = gather("vg_scales", v_scales, U8)
+        vg_words = gather("vg_words", v_words, U16)
+        go_mx = quantize("go", interleave("go", go_raw), Q)
+        c0 = product("c0", go_mx, vg_words, FP4X4, vg_scales, I)
+
+        p2 = tile("p2", [P, I + PAGE], F32)
+        z2 = tile("z2", [P, 1], F32)
+        nc.vector.scalar_tensor_tensor(
+            out=p2[:].rearrange("p (g j) -> p g j", j=PAGE), in0=gate[:].to_broadcast([P, G + 1, PAGE]), scalar=1.0,
+            in1=e[:].rearrange("p (g j) -> p g j", j=PAGE), op0=ALU.add, op1=ALU.mult, accum_out=z2[:])
+        w2 = tile("w2", [P, 1], F32)
+        nc.vector.reciprocal(w2[:], z2[:])
+        pn = tile("pn", [P, I], F32)
+        nc.scalar.activation(pn[:], p2[:, 0:I], ACT.Copy, scale=w2[:])
+
+        cp = tile("cp", [P, I], F32)
+        mean = tile("mean", [P, 1], F32)
+        nc.vector.scalar_tensor_tensor(out=cp[:], in0=c0[:], scalar=w2[:], in1=p2[:, 0:I],
+                                       op0=ALU.mult, op1=ALU.mult, accum_out=mean[:])
+        da = tile("da", [P, I], F32)
+        nc.vector.scalar_tensor_tensor(out=da[:], in0=c0[:], scalar=mean[:], in1=pn[:],
+                                       op0=ALU.subtract, op1=ALU.mult)
+        sq = tile("sq", [P, I], F32)
+        beta = tile("beta", [P, 1], F32)
+        nc.scalar.activation(sq[:], da[:], ACT.Square, scale=ROOT_K, accum_out=beta[:])
+        dap = tile("dap", [P, I], F32)
+        shift = tile("shift", [P, 1], F32)
+        nc.vector.scalar_tensor_tensor(out=dap[:], in0=da[:], scalar=-0.5 * ROOT_K, in1=pn[:],
+                                       op0=ALU.mult, op1=ALU.mult, accum_out=shift[:])
+        sq2 = tile("sq2", [P, I], F32)
+        nc.scalar.activation(sq2[:], da[:], ACT.Square, scale=ROOT_K, bias=shift[:])
+        rest = tile("rest", [P, I], F32)
+        nc.vector.scalar_tensor_tensor(out=rest[:], in0=pn[:], scalar=beta[:], in1=base_sb[:],
+                                       op0=ALU.mult, op1=ALU.subtract)
+        shift_sq = tile("shift_sq", [P, 1], F32)
+        nc.vector.tensor_tensor(shift_sq[:], shift[:], shift[:], ALU.mult)
+        y = tile("y", [P, I], F32)
+        nc.vector.scalar_tensor_tensor(out=y[:], in0=sq2[:], scalar=shift_sq[:], in1=rest[:],
+                                       op0=ALU.subtract, op1=ALU.subtract)
+        nc.sync.dma_start(out=out, in_=y[:])

@@ -28,24 +28,21 @@ def tile_attend_gppagetablegate_kernel(tc, query, pquery, keys_words, keys_scale
     nc = tc.nc
     with ExitStack() as ctx:
         sb = ctx.enter_context(tc.tile_pool(name="sb", bufs=1))
+        placed = ctx.enter_context(tc.tile_pool(name="placed", bufs=1))
         ps = ctx.enter_context(tc.psum_pool(name="ps", bufs=1))
 
-        def tile(name, shape, dtype):
-            return sb.tile(shape, dtype, name=name, align_bytes=64)
+        def tile(name, shape, dtype, on=None):
+            return sb.tile(shape, dtype, name=name, tag=on or name, align_bytes=64)
+
+        def place(name, shape, dtype, offset):
+            return placed.tile(shape, dtype, name=name, align_bytes=64, offset=offset)
 
         tokens = sb.tile([P, I // 16], U16, name="tokens")
         pages = sb.tile([P, G // 16], U16, name="pages")
         k_words = tile("k_words", [P, T], U16)
-        v_words = tile("v_words", [P, T], U16)
         k_scales = tile("k_scales", [P, T], U8)
-        v_scales = tile("v_scales", [P, T], U8)
-        q_raw = tile("q_raw", [P, PACK, Q], F32)
-        pq_raw = tile("pq_raw", [P, PACK, Q], F32)
-        go_raw = tile("go_raw", [P, PACK, Q], F32)
-        pg_raw = tile("pg_raw", [P, PACK * U], F32)
-        base_sb = tile("base_sb", [P, I], F32)
-        reserve_sb = tile("reserve_sb", [P, 1], F32)
         gate = tile("gate", [P, G + 1, 1], F32)
+        early = place("early", [P, 2560], F32, 2048)
 
         def load_scales(plane, scales, queue):
             rows = scales[0].bitcast(I32).rearrange("(s r) c -> r s c", r=4)
@@ -55,31 +52,36 @@ def tile_attend_gppagetablegate_kernel(tc, query, pquery, keys_words, keys_scale
         def planes(x):
             return x.rearrange("(p j) w -> p j w", j=PACK)
 
-        spread = tile("spread", [P, 1], F32)
         nc.vector.memset(k_scales[:].bitcast(I32), 0)
-        nc.vector.memset(spread[:], -0.75)
-        nc.vector.memset(v_scales[:].bitcast(I32), 0)
+        nc.vector.memset(early[:, 0:1], -0.75)
+        nc.scalar.activation(gate[:, G, :], early[:, 0:1], ACT.Copy)
+        pg_half = tile("pg_half", [P, 3 * U], BF16)
+        nc.vector.memset(pg_half[:, 2 * U:], 0.0)
         nc.sync.dma_start(tokens[:], offs)
-        nc.sync.dma_start(out=k_words[:].bitcast(I32), in_=keys_words[0].bitcast(I32))
-        load_scales(k_scales, keys_scales, nc.scalar)
-        nc.scalar.activation(gate[:, G, :], spread[:], ACT.Copy)
-        nc.sync.dma_start(out=pg_raw[:], in_=pgsum.rearrange("(p j) w -> p (j w)", j=PACK))
         nc.sync.dma_start(pages[:], offs2)
-        nc.sync.dma_start(out=pq_raw[:], in_=planes(pquery))
+        nc.sync.dma_start(out=k_words[:].bitcast(I32), in_=keys_words[0].bitcast(I32))
+        load_scales(k_scales, keys_scales, nc.sync)
+        q_raw = place("q_raw", [P, PACK, Q], F32, 0)
+        pq_raw = place("pq_raw", [P, PACK, Q], F32, 2048)
+        pg_raw = place("pg_raw", [P, PACK * U], F32, 4096)
+        go_raw = place("go_raw", [P, PACK, Q], F32, 8192)
         nc.sync.dma_start(out=q_raw[:], in_=planes(query))
-        load_scales(v_scales, vals_scales, nc.sync)
-        nc.sync.dma_start(out=v_words[:].bitcast(I32), in_=vals_words[0].bitcast(I32))
+        nc.sync.dma_start(out=pq_raw[:], in_=planes(pquery))
+        nc.sync.dma_start(out=pg_raw[:], in_=pgsum.rearrange("(p j) w -> p (j w)", j=PACK))
         nc.sync.dma_start(out=go_raw[:], in_=planes(gout))
-        nc.sync.dma_start(out=reserve_sb[:], in_=reserve)
-        nc.sync.dma_start(out=base_sb[:], in_=base)
+        v_scales = place("v_scales", [P, T], U8, 10240)
+        nc.vector.memset(v_scales[:].bitcast(I32), 0)
+        load_scales(v_scales, vals_scales, nc.sync)
 
-        def gather(name, window, dtype):
-            picked = tile(name, [P, I], dtype)
+        def gather(picked, window):
             nc.vector.tensor_copy(picked[:], window[:].indirect(tokens[:]))
             return picked
 
-        def quantize(name, grouped, width):
-            codes = tile(name + "_codes", [P, width], U32)
+        def quantize(name, grouped, width, offset=None):
+            if offset is None:
+                codes = tile(name + "_codes", [P, width], U32)
+            else:
+                codes = place(name + "_codes", [P, width], U32, offset)
             scales = tile(name + "_scales", [P, width], U8)
             nc.vector.quantize_mx(out=codes[:].bitcast(FP8X4), scales=scales[:],
                                   in_=grouped[:].rearrange("p w j -> p (w j)"))
@@ -87,8 +89,8 @@ def tile_attend_gppagetablegate_kernel(tc, query, pquery, keys_words, keys_scale
 
         def interleave(name, raw):
             grouped = tile(name + "_grouped", [P, Q, PACK], BF16)
-            nc.scalar.copy(out=grouped[:].rearrange("p (c i) j -> p c j i", i=4),
-                           in_=raw[:].rearrange("p j (c i) -> p c j i", i=4))
+            nc.scalar.activation(grouped[:].rearrange("p (c i) j -> p c j i", i=4),
+                                 raw[:].rearrange("p j (c i) -> p c j i", i=4), ACT.Copy)
             return grouped
 
         def product(name, rows, words, word_dtype, scales, width):
@@ -97,29 +99,37 @@ def tile_attend_gppagetablegate_kernel(tc, query, pquery, keys_words, keys_scale
                                 rhs=words[:].bitcast(word_dtype), rhs_scale=scales[:], start=True, stop=True)
             return acc
 
-        kg_scales = gather("kg_scales", k_scales, U8)
-        kg_words = gather("kg_words", k_words, U16)
-
-        pg_grouped = tile("pg_grouped", [P, G, PACK], BF16)
-        for j in range(PACK):
-            nc.vector.tensor_copy(pg_grouped[:, :, j], pg_raw[:, j * U:(j + 1) * U].indirect(pages[:]))
-        pg_codes, pg_scales = quantize("pg", pg_grouped, G)
-        pq_mx = quantize("pq", interleave("pq", pq_raw), Q)
-        h0 = product("h0", pq_mx, pg_codes, FP8X4, pg_scales, G)
-        nc.scalar.activation(gate[:, 0:G, 0], h0[:], ACT.Tanh, scale=0.5)
+        kg_words = gather(tile("kg_words", [P, I], U16), k_words)
+        kg_scales = gather(tile("kg_scales", [P, I], U8), k_scales)
+        v_words = tile("v_words", [P, T], U16, "k_words")
+        nc.sync.dma_start(out=v_words[:].bitcast(I32), in_=vals_words[0].bitcast(I32))
 
         q_mx = quantize("q", interleave("q", q_raw), Q)
         a = product("a", q_mx, kg_words, FP4X4, kg_scales, I)
-        e = tile("e", [P, I + PAGE], F32)
-        nc.scalar.activation(e[:, I:], reserve_sb[:].to_broadcast([P, PAGE]), ACT.Copy)
+        pq_mx = quantize("pq", interleave("pq", pq_raw), Q)
+
+        reserve_sb = place("reserve_sb", [P, 1], F32, 0)
+        base_sb = place("base_sb", [P, I], F32, 2048)
+        nc.sync.dma_start(out=reserve_sb[:], in_=reserve)
+        nc.sync.dma_start(out=base_sb[:], in_=base)
+        pg_grouped = tile("pg_grouped", [P, G, PACK], BF16)
+        nc.scalar.activation(pg_half[:, 0:2 * U], pg_raw[:, 2 * U:], ACT.Copy)
+        for j in range(2):
+            nc.scalar.activation(pg_grouped[:, :, 2 + j], pg_half[:, j * U:(j + 2) * U].indirect(pages[:]), ACT.Copy)
+            nc.vector.tensor_copy(pg_grouped[:, :, j], pg_raw[:, j * U:(j + 1) * U].indirect(pages[:]))
+        vg_scales = gather(place("vg_scales", [P, I], U8, 4096), v_scales)
+        pg_codes, pg_scales = quantize("pg", pg_grouped, G, 10240)
+        h0 = product("h0", pq_mx, pg_codes, FP8X4, pg_scales, G)
+        e = tile("e", [P, I + PAGE], F32, "pg_half")
         nc.scalar.activation(e[:, 0:I], a[:], ACT.Exp)
 
-        vg_scales = gather("vg_scales", v_scales, U8)
-        vg_words = gather("vg_words", v_words, U16)
-        go_mx = quantize("go", interleave("go", go_raw), Q)
+        go_mx = quantize("go", interleave("go", go_raw), Q, 11264)
+        vg_words = gather(tile("vg_words", [P, I], U16, "pg_grouped"), v_words)
         c0 = product("c0", go_mx, vg_words, FP4X4, vg_scales, I)
+        nc.scalar.activation(gate[:, 0:G, 0], h0[:], ACT.Tanh, scale=0.5)
+        nc.scalar.activation(e[:, I:], reserve_sb[:].to_broadcast([P, PAGE]), ACT.Copy)
 
-        p2 = tile("p2", [P, I + PAGE], F32)
+        p2 = tile("p2", [P, I + PAGE], F32, "k_words")
         z2 = tile("z2", [P, 1], F32)
         nc.vector.scalar_tensor_tensor(
             out=p2[:].rearrange("p (g j) -> p g j", j=PAGE), in0=gate[:].to_broadcast([P, G + 1, PAGE]), scalar=1.0,
@@ -143,14 +153,18 @@ def tile_attend_gppagetablegate_kernel(tc, query, pquery, keys_words, keys_scale
         shift = tile("shift", [P, 1], F32)
         nc.vector.scalar_tensor_tensor(out=dap[:], in0=da[:], scalar=-0.5 * ROOT_K, in1=pn[:],
                                        op0=ALU.mult, op1=ALU.mult, accum_out=shift[:])
-        sq2 = tile("sq2", [P, I], F32)
-        nc.scalar.activation(sq2[:], da[:], ACT.Square, scale=ROOT_K, bias=shift[:])
-        rest = tile("rest", [P, I], F32)
-        nc.vector.scalar_tensor_tensor(out=rest[:], in0=pn[:], scalar=beta[:], in1=base_sb[:],
-                                       op0=ALU.mult, op1=ALU.subtract)
         shift_sq = tile("shift_sq", [P, 1], F32)
-        nc.vector.tensor_tensor(shift_sq[:], shift[:], shift[:], ALU.mult)
+        halves = [slice(0, I // 2), slice(I // 2, I)]
+        sq2 = tile("sq2", [P, I], F32)
+        rest = tile("rest", [P, I], F32)
         y = tile("y", [P, I], F32)
-        nc.vector.scalar_tensor_tensor(out=y[:], in0=sq2[:], scalar=shift_sq[:], in1=rest[:],
-                                       op0=ALU.subtract, op1=ALU.subtract)
-        nc.sync.dma_start(out=out, in_=y[:])
+        for cols in halves:
+            nc.scalar.activation(sq2[:, cols], da[:, cols], ACT.Square, scale=ROOT_K, bias=shift[:])
+        nc.vector.tensor_tensor(shift_sq[:], shift[:], shift[:], ALU.mult)
+        for cols in halves:
+            nc.vector.scalar_tensor_tensor(out=rest[:, cols], in0=pn[:, cols], scalar=beta[:], in1=base_sb[:, cols],
+                                           op0=ALU.mult, op1=ALU.subtract)
+        for cols in halves:
+            nc.vector.scalar_tensor_tensor(out=y[:, cols], in0=sq2[:, cols], scalar=shift_sq[:], in1=rest[:, cols],
+                                           op0=ALU.subtract, op1=ALU.subtract)
+            nc.sync.dma_start(out=out[:, cols], in_=y[:, cols])

import math
from contextlib import ExitStack

import concourse.mybir as mybir

D, T, I, Q, G, U = 512, 2048, 512, 128, 64, 256
FLOPS = 2 * D * Q * (G + 2 * I)

F32 = mybir.dt.float32
BF16 = mybir.dt.bfloat16
I32 = mybir.dt.int32
U32 = mybir.dt.uint32
U16 = mybir.dt.uint16
U8 = mybir.dt.uint8
FP8X4 = mybir.dt.float8_e4m3fn_x4
FP4X4 = mybir.dt.float4_e2m1fn_x4
ALU = mybir.AluOpType
ACT = mybir.ActivationFunctionType

P = 128
PACK = 4
PAGE = I // G
ROOT_K = math.sqrt(512.0 * 2.0 * 512.0)


def tile_attend_gppagetablegate_kernel(tc, query, pquery, keys_words, keys_scales, pgsum, reserve, gout,
                                        vals_words, vals_scales, base, offs2, offs, out):
    nc = tc.nc
    with ExitStack() as ctx:
        sb = ctx.enter_context(tc.tile_pool(name="sb", bufs=1))
        placed = ctx.enter_context(tc.tile_pool(name="placed", bufs=1))
        ps = ctx.enter_context(tc.psum_pool(name="ps", bufs=1))

        def tile(name, shape, dtype, on=None):
            return sb.tile(shape, dtype, name=name, tag=on or name, align_bytes=64)

        def place(name, shape, dtype, offset):
            return placed.tile(shape, dtype, name=name, align_bytes=64, offset=offset)

        tokens = sb.tile([P, I // 16], U16, name="tokens")
        pages = sb.tile([P, G // 16], U16, name="pages")
        k_words = tile("k_words", [P, T], U16)
        k_scales = tile("k_scales", [P, T], U8)
        gate = tile("gate", [P, G + 1, 1], F32)
        early = place("early", [P, 2560], F32, 2048)

        def load_scales(plane, scales, queue):
            rows = scales[0].bitcast(I32).rearrange("(s r) c -> r s c", r=4)
            for r in range(4):
                queue.dma_start(out=plane[:].bitcast(I32)[r:P:32, :], in_=rows[r])

        def planes(x):
            return x.rearrange("(p j) w -> p j w", j=PACK)

        nc.vector.memset(k_scales[:].bitcast(I32), 0)
        nc.vector.memset(early[:, 0:1], -0.75)
        nc.scalar.activation(gate[:, G, :], early[:, 0:1], ACT.Copy)
        pg_half = tile("pg_half", [P, 3 * U], BF16)
        nc.vector.memset(pg_half[:, 2 * U:], 0.0)
        nc.sync.dma_start(tokens[:], offs)
        nc.sync.dma_start(pages[:], offs2)
        nc.sync.dma_start(out=k_words[:].bitcast(I32), in_=keys_words[0].bitcast(I32))
        load_scales(k_scales, keys_scales, nc.sync)
        q_raw = place("q_raw", [P, PACK, Q], F32, 0)
        pq_raw = place("pq_raw", [P, PACK, Q], F32, 2048)
        pg_raw = place("pg_raw", [P, PACK * U], F32, 4096)
        go_raw = place("go_raw", [P, PACK, Q], F32, 8192)
        nc.sync.dma_start(out=q_raw[:], in_=planes(query))
        nc.sync.dma_start(out=pq_raw[:], in_=planes(pquery))
        nc.sync.dma_start(out=pg_raw[:], in_=pgsum.rearrange("(p j) w -> p (j w)", j=PACK))
        nc.sync.dma_start(out=go_raw[:], in_=planes(gout))
        v_scales = place("v_scales", [P, T], U8, 10240)
        nc.vector.memset(v_scales[:].bitcast(I32), 0)
        load_scales(v_scales, vals_scales, nc.sync)

        def gather(picked, window):
            nc.vector.tensor_copy(picked[:], window[:].indirect(tokens[:]))
            return picked

        def quantize(name, grouped, width, offset=None):
            if offset is None:
                codes = tile(name + "_codes", [P, width], U32)
            else:
                codes = place(name + "_codes", [P, width], U32, offset)
            scales = tile(name + "_scales", [P, width], U8)
            nc.vector.quantize_mx(out=codes[:].bitcast(FP8X4), scales=scales[:],
                                  in_=grouped[:].rearrange("p w j -> p (w j)"))
            return codes, scales

        def interleave(name, raw):
            grouped = tile(name + "_grouped", [P, Q, PACK], BF16)
            nc.scalar.activation(grouped[:].rearrange("p (c i) j -> p c j i", i=4),
                                 raw[:].rearrange("p j (c i) -> p c j i", i=4), ACT.Copy)
            return grouped

        def product(name, rows, words, word_dtype, scales, width):
            acc = ps.tile([P, width], F32, name=name)
            nc.tensor.matmul_mx(out=acc[:], lhsT=rows[0][:].bitcast(FP8X4), lhsT_scale=rows[1][:],
                                rhs=words[:].bitcast(word_dtype), rhs_scale=scales[:], start=True, stop=True)
            return acc

        kg_words = gather(tile("kg_words", [P, I], U16), k_words)
        kg_scales = gather(tile("kg_scales", [P, I], U8), k_scales)
        v_words = tile("v_words", [P, T], U16, "k_words")
        nc.sync.dma_start(out=v_words[:].bitcast(I32), in_=vals_words[0].bitcast(I32))

        q_mx = quantize("q", interleave("q", q_raw), Q)
        a = product("a", q_mx, kg_words, FP4X4, kg_scales, I)
        pq_mx = quantize("pq", interleave("pq", pq_raw), Q)

        reserve_sb = place("reserve_sb", [P, 1], F32, 0)
        base_sb = place("base_sb", [P, I], F32, 2048)
        nc.sync.dma_start(out=reserve_sb[:], in_=reserve)
        nc.sync.dma_start(out=base_sb[:], in_=base)
        pg_grouped = tile("pg_grouped", [P, G, PACK], BF16)
        nc.scalar.activation(pg_half[:, 0:2 * U], pg_raw[:, 2 * U:], ACT.Copy)
        for j in range(2):
            nc.scalar.activation(pg_grouped[:, :, 2 + j], pg_half[:, j * U:(j + 2) * U].indirect(pages[:]), ACT.Copy)
            nc.vector.tensor_copy(pg_grouped[:, :, j], pg_raw[:, j * U:(j + 1) * U].indirect(pages[:]))
        vg_scales = gather(place("vg_scales", [P, I], U8, 4096), v_scales)
        pg_codes, pg_scales = quantize("pg", pg_grouped, G, 10240)
        h0 = product("h0", pq_mx, pg_codes, FP8X4, pg_scales, G)
        e = tile("e", [P, I + PAGE], F32, "pg_half")
        nc.scalar.activation(e[:, 0:I], a[:], ACT.Exp)

        go_mx = quantize("go", interleave("go", go_raw), Q, 11264)
        vg_words = gather(tile("vg_words", [P, I], U16, "pg_grouped"), v_words)
        c0 = product("c0", go_mx, vg_words, FP4X4, vg_scales, I)
        nc.scalar.activation(gate[:, 0:G, 0], h0[:], ACT.Tanh, scale=0.5)
        nc.scalar.activation(e[:, I:], reserve_sb[:].to_broadcast([P, PAGE]), ACT.Copy)

        p2 = tile("p2", [P, I + PAGE], F32, "k_words")
        z2 = tile("z2", [P, 1], F32)
        nc.vector.scalar_tensor_tensor(
            out=p2[:].rearrange("p (g j) -> p g j", j=PAGE), in0=gate[:].to_broadcast([P, G + 1, PAGE]), scalar=1.0,
            in1=e[:].rearrange("p (g j) -> p g j", j=PAGE), op0=ALU.add, op1=ALU.mult, accum_out=z2[:])
        w2 = tile("w2", [P, 1], F32)
        nc.vector.reciprocal(w2[:], z2[:])
        pn = tile("pn", [P, I], F32)
        nc.scalar.activation(pn[:], p2[:, 0:I], ACT.Copy, scale=w2[:])

        cp = tile("cp", [P, I], F32)
        mean = tile("mean", [P, 1], F32)
        nc.vector.scalar_tensor_tensor(out=cp[:], in0=c0[:], scalar=w2[:], in1=p2[:, 0:I],
                                       op0=ALU.mult, op1=ALU.mult, accum_out=mean[:])
        da = tile("da", [P, I], F32)
        nc.vector.scalar_tensor_tensor(out=da[:], in0=c0[:], scalar=mean[:], in1=pn[:],
                                       op0=ALU.subtract, op1=ALU.mult)
        sq = tile("sq", [P, I], F32)
        beta = tile("beta", [P, 1], F32)
        nc.scalar.activation(sq[:], da[:], ACT.Square, scale=ROOT_K, accum_out=beta[:])
        dap = tile("dap", [P, I], F32)
        shift = tile("shift", [P, 1], F32)
        nc.vector.scalar_tensor_tensor(out=dap[:], in0=da[:], scalar=-0.5 * ROOT_K, in1=pn[:],
                                       op0=ALU.mult, op1=ALU.mult, accum_out=shift[:])
        shift_sq = tile("shift_sq", [P, 1], F32)
        halves = [slice(0, I // 2), slice(I // 2, I)]
        sq2 = tile("sq2", [P, I], F32)
        rest = tile("rest", [P, I], F32)
        y = tile("y", [P, I], F32)
        for cols in halves:
            nc.scalar.activation(sq2[:, cols], da[:, cols], ACT.Square, scale=ROOT_K, bias=shift[:])
        nc.vector.tensor_tensor(shift_sq[:], shift[:], shift[:], ALU.mult)
        for cols in halves:
            nc.vector.scalar_tensor_tensor(out=rest[:, cols], in0=pn[:, cols], scalar=beta[:], in1=base_sb[:, cols],
                                           op0=ALU.mult, op1=ALU.subtract)
        for cols in halves:
            nc.vector.scalar_tensor_tensor(out=y[:, cols], in0=sq2[:, cols], scalar=shift_sq[:], in1=rest[:, cols],
                                           op0=ALU.subtract, op1=ALU.subtract)
            nc.sync.dma_start(out=out[:, cols], in_=y[:, cols])
